import numpy as np
import ml_dtypes


def mxq(x, axis, fmt="e4m3"):
    dtype, down = {"e4m3": (ml_dtypes.float8_e4m3fn, 7), "e5m2": (ml_dtypes.float8_e5m2, 14)}[fmt]
    v = np.moveaxis(np.asarray(x, np.float32).astype(ml_dtypes.bfloat16).astype(np.float64), axis, -1)
    blocks = v.reshape(v.shape[:-1] + (-1, 32))
    amax = np.abs(blocks).max(-1, keepdims=True)
    byte = np.maximum(np.where(amax > 0, np.frexp(amax)[1] - 1 + 127, 0) - down, 1)
    scale = np.exp2(byte - 127.0)
    codes = (blocks / scale).astype(np.float32).astype(dtype).astype(np.float64)
    return np.moveaxis((codes * scale).reshape(v.shape), -1, axis)


WIDE = False


def mx_kscale(k):
    if not WIDE:
        return np.ones(k)
    levels = np.array([10, -10, 5, -5, 0])
    if k % 512:
        return np.exp2(np.random.permutation(np.resize(levels, k // 32))).repeat(32)
    a = np.empty((k // 512, 16))
    for p in range(k // 512):
        a[p, :8] = np.random.permutation(np.resize(levels, 8))
        for g in range(8):
            far = levels[np.abs(levels - a[p, g]) >= 10]
            a[p, g + 8] = far[np.random.randint(len(far))]
    return np.exp2(a.ravel()).repeat(32)


def f64(x):
    return np.asarray(x).astype(np.float64)


def striped(idx):
    return np.tile(idx.reshape(-1, 16).T, (8, 1)).astype(np.uint16)


def unstriped(offs):
    return offs[:16].T.reshape(-1).astype(np.int64)


E2M1 = np.array([0.0, 0.5, 1.0, 1.5, 2.0, 3.0, 4.0, 6.0, -0.0, -0.5, -1.0, -1.5, -2.0, -3.0, -4.0, -6.0])


def pack_weight(w, fmt):
    k, n = w.shape
    w = f64(np.asarray(w, np.float32).astype(ml_dtypes.bfloat16)).reshape(k // 32, 32, n)
    amax = np.abs(w).max(1)
    if fmt == "e4m3":
        byte = np.frexp(amax)[1] - 1 + 127 - 7
    else:
        mant, ex = np.frexp(amax / 6.0)
        byte = np.where(mant > 0.5, ex, ex - 1) + 127
    byte = np.clip(np.where(amax > 0, byte, 1), 1, 254)
    scaled = (w * np.exp2(127.0 - byte)[:, None, :]).reshape(k, n).astype(np.float32)
    by_word = np.ascontiguousarray(scaled.reshape(k // 512, 128, 4, n).transpose(0, 1, 3, 2))
    if fmt == "e4m3":
        words = by_word.astype(ml_dtypes.float8_e4m3fn).view(np.uint8)
    else:
        c = by_word.astype(ml_dtypes.float4_e2m1fn).view(np.uint8) & 0xF
        words = (c[..., 0::2] | (c[..., 1::2] << 4)).reshape(k // 512, 128, 2 * n)
    return np.ascontiguousarray(words), np.ascontiguousarray(byte.astype(np.uint8).reshape(k // 512, 16, n))


def unpack_weight(words, scales, fmt):
    g, _, n = scales.shape
    words = np.ascontiguousarray(words).reshape(g, 128, n, -1)
    if fmt == "e4m3":
        vals = words.view(ml_dtypes.float8_e4m3fn).astype(np.float64)
    else:
        nib = np.empty((g, 128, n, 4), np.uint8)
        nib[..., 0::2] = words & 0xF
        nib[..., 1::2] = words >> 4
        vals = E2M1[nib]
    vals = vals * np.repeat(np.exp2(scales.astype(np.float64) - 127.0), 8, axis=1)[..., None]
    return vals.transpose(0, 1, 3, 2).reshape(g * 512, n)


def gelu(v):
    return 0.5 * v * (1.0 + np.tanh(np.sqrt(2.0 / np.pi) * (v + 0.044715 * v**3)))


def bf(x):
    return np.asarray(x, np.float32).astype(ml_dtypes.bfloat16)


def planes(Y):
    n, m = Y.shape
    b = f64(bf(Y)).reshape(n // 32, 32, m)
    amax = np.abs(b).max(1)
    byte = np.clip(np.where(amax > 0, np.frexp(amax)[1] - 1 + 127 - 7, 1), 1, 254)
    codes = (b * np.exp2(127.0 - byte)[:, None, :]).reshape(n, m).astype(np.float32).astype(ml_dtypes.float8_e4m3fn).view(np.uint8)
    words = codes.reshape(n // 512, 128, 4, m).transpose(0, 1, 3, 2)
    return np.ascontiguousarray(words), np.ascontiguousarray(byte.astype(np.uint8).reshape(n // 512, 16, m))


K, T, S, H, P, N, P2 = 1024, 4096, 1024, 1024, 512, 1024, 256


def setup_inputs():
    n = np.random.standard_normal
    s = mx_kscale(K)[:, None]
    u = mx_kscale(H)[:, None]
    tab_words, tab_scales = pack_weight(n((K, T)) * s, "e4m3")
    w4 = n((H, N)) / np.sqrt(H) * np.exp(0.8 * n(N))[None, :] / u
    w4_words, w4_scales = pack_weight(w4, "e2m1")
    return {
        "tab_words": tab_words, "tab_scales": tab_scales,
        "offs": striped(np.random.permutation(T)[:S]),
        "pos1": striped(np.random.permutation(S)[:P]),
        "pos2": striped(np.random.permutation(S)[:P]),
        "pos3": striped(np.random.permutation(P)[:P2]),
        "pos4": striped(np.random.permutation(P)[:P2]),
        "w1": (0.42 * n((K, H)) / np.sqrt(K) / s).astype(np.float32),
        "b1": np.random.uniform(-0.6, 0.6, H).astype(np.float32),
        "gain": (2.0 * np.exp(0.3 * n(H)) * np.sqrt(u[:, 0])).astype(np.float32),
        "w4_words": w4_words, "w4_scales": w4_scales,
        "sister": (0.4 * np.exp(0.3 * n(N))).astype(np.float32),
    }


def reference(tab_words, tab_scales, offs, pos1, pos2, pos3, pos4, w1, b1, gain,
              w4_words, w4_scales, sister):
    v = unpack_weight(tab_words, tab_scales, "e4m3")[:, unstriped(offs)]
    w4 = unpack_weight(w4_words, w4_scales, "e2m1")
    tone = (mxq(f64(w1), 0, "e4m3").T @ v) + f64(b1)[:, None]
    h = f64(gain)[:, None] * np.sin(tone)
    z = h[:, unstriped(pos1)] * h[:, unstriped(pos2)]
    f = w4.T @ mxq(z, 0, "e4m3")
    y = np.tanh(f[:, unstriped(pos3)]) + f64(sister)[:, None] * f[:, unstriped(pos4)]
    words, scales = planes(y)
    return y, words, scales

@@ -1,0 +1,278 @@
+import math
+from contextlib import ExitStack
+
+import concourse.mybir as mybir
+
+K, T, S, H, M, N, J = 1024, 4096, 1024, 1024, 512, 1024, 256
+FLOPS = 2 * K * H * S + 2 * H * N * M
+
+F32 = mybir.dt.float32
+BF16 = mybir.dt.bfloat16
+I32 = mybir.dt.int32
+U32 = mybir.dt.uint32
+U16 = mybir.dt.uint16
+U8 = mybir.dt.uint8
+FP8X4 = mybir.dt.float8_e4m3fn_x4
+FP4X4 = mybir.dt.float4_e2m1fn_x4
+ACT = mybir.ActivationFunctionType
+ALU = mybir.AluOpType
+
+P = 128
+PACK = 4
+PASS = P * PACK
+BANK = 512
+QUADS = 4
+TWO_PI = 2.0 * math.pi
+ROUNDER = 1.5 * 2.0**23
+W1_VECTOR_COLS = 88
+
+
+def tile_list_hive_clip_board_kernel(tc, tab_words, tab_scales, offs, pos1, pos2, pos3, pos4, w1, b1, gain,
+                                                w4_words, w4_scales, sister, out_0, out_1, out_2):
+    nc = tc.nc
+    with ExitStack() as ctx:
+        keep = ctx.enter_context(tc.tile_pool(name="keep", bufs=1))
+        ring = ctx.enter_context(tc.tile_pool(name="ring", bufs=2))
+        psum = ctx.enter_context(tc.psum_pool(name="psum", bufs=8))
+
+        def load_list(src, name):
+            tile = keep.tile(list(src.shape), U16, name=name)
+            nc.sync.dma_start(tile[:], src)
+            return tile
+
+        def load_rows(src, name):
+            tile = keep.tile([P, 2, PACK], F32, name=name)
+            nc.gpsimd.dma_start(tile[:], src.rearrange("(b p t) -> p b t", p=P, t=PACK))
+            return tile
+
+        def load_w1(a, b):
+            raw = keep.tile([P, PACK, PASS], F32, name="w1_raw_%d%d" % (a, b))
+            rows = w1[a * PASS : (a + 1) * PASS, b * PASS : (b + 1) * PASS]
+            nc.sync.dma_start(raw[:], rows.rearrange("(p j) c -> p j c", j=PACK))
+            return raw
+
+        table_sc = keep.tile([P, T], U8)
+        nc.vector.memset(table_sc[:].bitcast(I32), 0)
+        offs_sb = load_list(offs, "offs_sb")
+        for q in range(QUADS):
+            nc.scalar.dma_start(table_sc[32 * q : 32 * q + 8, :].bitcast(I32),
+                                tab_scales[:, 4 * q : 4 * q + 4, :].bitcast(I32))
+        table = []
+        for a in range(2):
+            words = keep.tile([P, T], I32, name="table_%d" % a)
+            nc.sync.dma_start(words[:], tab_words[a].rearrange("p t i -> p (t i)").bitcast(I32))
+            table.append(words)
+        w1_raw = {(a, 0): load_w1(a, 0) for a in range(2)}
+        w4_raw = keep.tile([P, 2, 2 * N], U8)
+        nc.sync.dma_start(w4_raw[:].bitcast(I32), w4_words.rearrange("a p c -> p a c").bitcast(I32))
+        pos1_sb = load_list(pos1, "pos1_sb")
+        pos2_sb = load_list(pos2, "pos2_sb")
+        for a in range(2):
+            w1_raw[(a, 1)] = load_w1(a, 1)
+        pos3_sb = load_list(pos3, "pos3_sb")
+        pos4_sb = load_list(pos4, "pos4_sb")
+
+        w4_sc_raw = keep.tile([P, 2, N], U8)
+        nc.vector.memset(w4_sc_raw[:].bitcast(I32), 0)
+        gain_sb = load_rows(gain, "gain_sb")
+        b1_sb = load_rows(b1, "b1_sb")
+        for q in range(QUADS):
+            nc.gpsimd.dma_start(w4_sc_raw[32 * q : 32 * q + 4, :, :].bitcast(I32),
+                                w4_scales[:, 4 * q : 4 * q + 4, :].rearrange("a r n -> r a n").bitcast(I32))
+        sister_sb = load_rows(sister, "sister_sb")
+
+        gain2 = []
+        for i in range(2 * PACK):
+            spread = keep.tile([P, M], F32, name="gain2_%d" % i)
+            column = gain_sb[:, i // PACK, i % PACK : i % PACK + 1]
+            nc.scalar.activation(spread[:], column.to_broadcast([P, M]), ACT.Square)
+            gain2.append(spread)
+        b1_turns = keep.tile([P, 2, PACK], F32)
+        nc.scalar.activation(b1_turns[:], b1_sb[:], ACT.Copy, scale=1.0 / TWO_PI)
+
+        picked = [keep.tile([P, S], U32, name="picked_%d" % a, align_bytes=64) for a in range(2)]
+        picked_sc = keep.tile([P, S], U8, align_bytes=64)
+        nc.vector.tensor_copy(picked[0][:], table[0][:].bitcast(U32).indirect(offs_sb[:]))
+        nc.vector.tensor_copy(picked_sc[:], table_sc[:].indirect(offs_sb[:]))
+        nc.vector.tensor_copy(picked[1][:], table[1][:].bitcast(U32).indirect(offs_sb[:]))
+
+        w4_sc = keep.tile([P, 2, N], U8, align_bytes=64)
+        nc.vector.tensor_copy(
+            w4_sc[:].rearrange("p a (g t c i) -> p (a g) c t i", g=2, t=PACK, i=16),
+            w4_sc_raw[:].rearrange("p a (g c i t) -> p (a g) c t i", g=2, t=PACK, i=16))
+
+        w1_bf = {}
+        w1_codes = {}
+        w1_sc = {}
+
+        def round_w1(a, b):
+            dealt = ring.tile([P, PACK, P, PACK], BF16, name="w1_dealt", align_bytes=64)
+            src = w1_raw[(a, b)][:].rearrange("p j (m t) -> p m t j", t=PACK)
+            dst = dealt[:].rearrange("p t m j -> p m t j")
+            nc.vector.tensor_copy(dst[:, :W1_VECTOR_COLS], src[:, :W1_VECTOR_COLS])
+            nc.scalar.copy(dst[:, W1_VECTOR_COLS:], src[:, W1_VECTOR_COLS:])
+            w1_bf[(a, b)] = dealt
+
+        def quantise_w1(a, b, pieces):
+            codes = keep.tile([P, PASS], U32, name="w1_codes_%d%d" % (a, b), align_bytes=64)
+            scales = keep.tile([P, PASS], U8, name="w1_sc_%d%d" % (a, b), align_bytes=64)
+            flat = w1_bf[(a, b)][:].rearrange("p t m j -> p (t m j)")
+            width = PASS // pieces
+            for c in range(0, PASS, width):
+                nc.vector.quantize_mx(codes[:, c : c + width].bitcast(FP8X4), scales[:, c : c + width],
+                                      flat[:, PACK * c : PACK * (c + width)])
+            w1_codes[(a, b)] = codes
+            w1_sc[(a, b)] = scales
+
+        round_w1(0, 0)
+        quantise_w1(0, 0, 1)
+        round_w1(1, 0)
+        quantise_w1(1, 0, PACK)
+
+        w4_dealt = keep.tile([P, 2, 2 * N], U8, align_bytes=64)
+        nc.vector.tensor_copy(
+            w4_dealt[:].bitcast(U16).rearrange("p a (g t c i) -> p (a g) c t i", g=2, t=PACK, i=8),
+            w4_raw[:].bitcast(U16).rearrange("p a (g c i t) -> p (a g) c t i", g=2, t=PACK, i=8))
+
+        turns, wholes, fracs, sines = {}, {}, {}, {}
+        z_f32 = [keep.tile([P, PACK, M], F32, name="z_f32_%d" % b) for b in range(2)]
+        z_bf = [keep.tile([P, M, PACK], BF16, name="z_bf_%d" % b, align_bytes=64) for b in range(2)]
+        z_codes = [keep.tile([P, M], U32, name="z_codes_%d" % b, align_bytes=64) for b in range(2)]
+        z_sc = [keep.tile([P, M], U8, name="z_sc_%d" % b, align_bytes=64) for b in range(2)]
+
+        def product1(i):
+            b, t = divmod(i, PACK)
+            turn = ring.tile([P, S], F32, name="turn", bufs=3)
+            for c in range(0, S, BANK):
+                bank = psum.tile([P, BANK], F32, name="bank")
+                for a in range(2):
+                    nc.tensor.matmul_mx(
+                        bank[:],
+                        lhsT=w1_codes[(a, b)][:, t * P : (t + 1) * P].bitcast(FP8X4),
+                        lhsT_scale=w1_sc[(a, b)][:, t * P : (t + 1) * P],
+                        rhs=picked[a][:, c : c + BANK].bitcast(FP8X4),
+                        rhs_scale=picked_sc[4 * a :, c : c + BANK],
+                        start=(a == 0), stop=(a == 1))
+                nc.scalar.activation(turn[:, c : c + BANK], bank[:], ACT.Identity,
+                                     bias=b1_turns[:, b, t : t + 1], scale=1.0 / TWO_PI)
+            turns[i] = turn
+
+        def new_tiles(i):
+            wholes[i] = ring.tile([P, S], I32, name="whole")
+            fracs[i] = ring.tile([P, S], F32, name="frac")
+            sines[i] = ring.tile([P, S], F32, name="sine")
+
+        def whole_turns(i, cols, on_vector):
+            if on_vector:
+                nc.vector.tensor_scalar(wholes[i][:, cols], turns[i][:, cols], ROUNDER, None, ALU.add)
+            else:
+                nc.scalar.activation(wholes[i][:, cols].bitcast(U32), turns[i][:, cols], ACT.Copy, bias=ROUNDER)
+
+        def fraction(i, cols):
+            nc.vector.scalar_tensor_tensor(fracs[i][:, cols], wholes[i][:, cols], ROUNDER, turns[i][:, cols],
+                                           ALU.subtract, ALU.subtract)
+
+        def sine(i, cols):
+            nc.scalar.activation(sines[i][:, cols], fracs[i][:, cols], ACT.Sin, scale=-TWO_PI)
+
+        def pairs(i, lo, hi):
+            b, t = divmod(i, PACK)
+            dusk = ring.tile([P, hi - lo], F32, name="dusk")
+            nc.vector.tensor_tensor(dusk[:], sines[i][:].indirect(pos1_sb[:, lo // 16 : hi // 16]),
+                                    gain2[i][:, lo:hi], ALU.mult)
+            nc.vector.tensor_tensor(z_f32[b][:, t, lo:hi], sines[i][:].indirect(pos2_sb[:, lo // 16 : hi // 16]),
+                                    dusk[:], ALU.mult)
+
+        def weave(copy, dst, src, lo, hi):
+            copy(dst[:, lo:hi, :].rearrange("p (c i) t -> p c t i", i=4),
+                 src[:, :, lo:hi].rearrange("p t (c i) -> p c t i", i=4))
+
+        def quantise(codes, scales, src, lo, hi):
+            nc.vector.quantize_mx(codes[:, lo:hi].bitcast(FP8X4), scales[:, lo:hi],
+                                  src[:, lo:hi, :].rearrange("p m t -> p (m t)"))
+
+        everything = slice(0, S)
+        tiles = 2 * PACK
+        product1(0)
+        new_tiles(0)
+        for c in range(0, S, BANK):
+            whole_turns(0, slice(c, c + BANK), True)
+            fraction(0, slice(c, c + BANK))
+        for i in range(tiles):
+            if i + 1 < tiles:
+                product1(i + 1)
+                new_tiles(i + 1)
+                whole_turns(i + 1, everything, False)
+            if i == 0:
+                for c in range(0, S, BANK):
+                    sine(0, slice(c, c + BANK))
+            else:
+                sine(i, everything)
+            if i + 1 < tiles:
+                fraction(i + 1, everything)
+            if i in (0, 1):
+                round_w1(i, 1)
+            if i + 1 < tiles:
+                pairs(i, 0, M)
+            if i in (0, 1):
+                quantise_w1(i, 1, 1)
+            if i >= PACK:
+                piece = M // PACK
+                weave(nc.scalar.copy, z_bf[0], z_f32[0], (i - PACK) * piece, (i - PACK + 1) * piece)
+        half = M // 2
+        pairs(tiles - 1, 0, half)
+        weave(nc.scalar.copy, z_bf[1], z_f32[1], 0, half)
+        quantise(z_codes[0], z_sc[0], z_bf[0], 0, M)
+        pairs(tiles - 1, half, M)
+        quantise(z_codes[1], z_sc[1], z_bf[1], 0, half)
+        weave(nc.vector.tensor_copy, z_bf[1], z_f32[1], half, M)
+        quantise(z_codes[1], z_sc[1], z_bf[1], half, M)
+
+        y_f32 = [keep.tile([P, PACK, J], F32, name="y_f32_%d" % g) for g in range(2)]
+        y_bf = [keep.tile([P, J, PACK], BF16, name="y_bf_%d" % g, align_bytes=64) for g in range(2)]
+        y_codes = [keep.tile([P, J], U32, name="y_codes_%d" % g, align_bytes=64) for g in range(2)]
+        y_sc = keep.tile([P, 2, J], U8, align_bytes=64)
+        bent, scaled = {}, {}
+
+        def product2(i):
+            g, t = divmod(i, PACK)
+            bank = psum.tile([P, BANK], F32, name="bank")
+            c = g * PASS + t * P
+            for b in range(2):
+                nc.tensor.matmul_mx(
+                    bank[:],
+                    lhsT=w4_dealt[:, b, 2 * c : 2 * (c + P)].bitcast(FP4X4),
+                    lhsT_scale=w4_sc[:, b, c : c + P],
+                    rhs=z_codes[b][:].bitcast(FP8X4),
+                    rhs_scale=z_sc[b][:],
+                    start=(b == 0), stop=(b == 1))
+            bent[i] = ring.tile([P, M], F32, name="bent", bufs=3)
+            scaled[i] = ring.tile([P, M], F32, name="scaled", bufs=3)
+            nc.scalar.activation(bent[i][:], bank[:], ACT.Tanh)
+            nc.scalar.activation(scaled[i][:], bank[:], ACT.Copy, scale=sister_sb[:, g, t : t + 1])
+
+        def colonies(i):
+            g, t = divmod(i, PACK)
+            colony = ring.tile([P, J], F32, name="colony")
+            nc.vector.tensor_copy(colony[:], bent[i][:].indirect(pos3_sb[:]))
+            nc.vector.tensor_tensor(y_f32[g][:, t, :], scaled[i][:].indirect(pos4_sb[:]), colony[:], ALU.add)
+            rows = out_0[g * PASS : (g + 1) * PASS, :].rearrange("(p t) j -> p t j", t=PACK)
+            nc.sync.dma_start(rows[:, t, :], y_f32[g][:, t, :])
+
+        def planes(g, copy):
+            weave(copy, y_bf[g], y_f32[g], 0, J)
+            quantise(y_codes[g], y_sc[:, g, :], y_bf[g], 0, J)
+            nc.sync.dma_start(out_1[g].rearrange("p m t -> p (m t)").bitcast(I32), y_codes[g][:].bitcast(I32))
+
+        product2(0)
+        for i in range(tiles):
+            if i + 1 < tiles:
+                product2(i + 1)
+            colonies(i)
+            if i == PACK:
+                planes(0, nc.scalar.copy)
+        planes(1, nc.vector.tensor_copy)
+        for q in range(QUADS):
+            queue = nc.scalar if q % 2 else nc.sync
+            queue.dma_start(out_2[:, 4 * q : 4 * q + 4, :].rearrange("g r m -> r g m").bitcast(I32),
+                            y_sc[32 * q : 32 * q + 4, :, :].bitcast(I32))

@@ -24,7 +24,7 @@ BANK = 512
 QUADS = 4
 TWO_PI = 2.0 * math.pi
 ROUNDER = 1.5 * 2.0**23
-W1_VECTOR_COLS = 88
+W1_VECTOR_COLS = (88, 96)
 
 
 def tile_list_hive_clip_board_kernel(tc, tab_words, tab_scales, offs, pos1, pos2, pos3, pos4, w1, b1, gain,
@@ -42,48 +42,53 @@ def tile_list_hive_clip_board_kernel(tc, tab_words, tab_scales, offs, pos1, pos2
 
         def load_rows(src, name):
             tile = keep.tile([P, 2, PACK], F32, name=name)
-            nc.gpsimd.dma_start(tile[:], src.rearrange("(b p t) -> p b t", p=P, t=PACK))
+            nc.sync.dma_start(tile[:], src.rearrange("(b p t) -> p b t", p=P, t=PACK))
             return tile
 
+        def load_table(a, half):
+            cols = slice(half * T // 2, (half + 1) * T // 2)
+            nc.sync.dma_start(table[a][:, cols], tab_words[a].rearrange("p t i -> p (t i)").bitcast(I32)[:, cols])
+
         def load_w1(a, b):
-            raw = keep.tile([P, PACK, PASS], F32, name="w1_raw_%d%d" % (a, b))
+            raw = keep.tile([P, PACK, PASS], F32, name="w1_raw_%d%d" % (a, b), tag="w1_raw_%d%d" % (a, b))
             rows = w1[a * PASS : (a + 1) * PASS, b * PASS : (b + 1) * PASS]
             nc.sync.dma_start(raw[:], rows.rearrange("(p j) c -> p j c", j=PACK))
             return raw
 
         table_sc = keep.tile([P, T], U8)
-        nc.vector.memset(table_sc[:].bitcast(I32), 0)
-        offs_sb = load_list(offs, "offs_sb")
-        for q in range(QUADS):
-            nc.scalar.dma_start(table_sc[32 * q : 32 * q + 8, :].bitcast(I32),
-                                tab_scales[:, 4 * q : 4 * q + 4, :].bitcast(I32))
-        table = []
-        for a in range(2):
-            words = keep.tile([P, T], I32, name="table_%d" % a)
-            nc.sync.dma_start(words[:], tab_words[a].rearrange("p t i -> p (t i)").bitcast(I32))
-            table.append(words)
-        w1_raw = {(a, 0): load_w1(a, 0) for a in range(2)}
-        w4_raw = keep.tile([P, 2, 2 * N], U8)
-        nc.sync.dma_start(w4_raw[:].bitcast(I32), w4_words.rearrange("a p c -> p a c").bitcast(I32))
-        pos1_sb = load_list(pos1, "pos1_sb")
-        pos2_sb = load_list(pos2, "pos2_sb")
-        for a in range(2):
-            w1_raw[(a, 1)] = load_w1(a, 1)
-        pos3_sb = load_list(pos3, "pos3_sb")
-        pos4_sb = load_list(pos4, "pos4_sb")
-
         w4_sc_raw = keep.tile([P, 2, N], U8)
+        nc.vector.memset(table_sc[:, : T // 2].bitcast(I32), 0)
+        nc.gpsimd.memset(table_sc[:, T // 2 :].bitcast(I32), 0)
         nc.vector.memset(w4_sc_raw[:].bitcast(I32), 0)
+        table = [keep.tile([P, T], I32, name="table_%d" % a, tag="table_%d" % a, align_bytes=64) for a in range(2)]
+        w1_raw = {(0, 0): load_w1(0, 0)}
+        offs_sb = load_list(offs, "offs_sb")
         gain_sb = load_rows(gain, "gain_sb")
         b1_sb = load_rows(b1, "b1_sb")
-        for q in range(QUADS):
-            nc.gpsimd.dma_start(w4_sc_raw[32 * q : 32 * q + 4, :, :].bitcast(I32),
-                                w4_scales[:, 4 * q : 4 * q + 4, :].rearrange("a r n -> r a n").bitcast(I32))
         sister_sb = load_rows(sister, "sister_sb")
+        pos1_sb = load_list(pos1, "pos1_sb")
+        pos2_sb = load_list(pos2, "pos2_sb")
+        load_table(0, 0)
+        pos3_sb = load_list(pos3, "pos3_sb")
+        pos4_sb = load_list(pos4, "pos4_sb")
+        for q in range(QUADS):
+            nc.sync.dma_start(table_sc[32 * q : 32 * q + 8, :].bitcast(I32),
+                              tab_scales[:, 4 * q : 4 * q + 4, :].bitcast(I32))
+        load_table(0, 1)
+        load_table(1, 0)
+        for q in range(QUADS):
+            nc.sync.dma_start(w4_sc_raw[32 * q : 32 * q + 4, :, :].bitcast(I32),
+                              w4_scales[:, 4 * q : 4 * q + 4, :].rearrange("a r n -> r a n").bitcast(I32))
+        load_table(1, 1)
+        w1_raw[(1, 0)] = load_w1(1, 0)
+        w4_raw = keep.tile([P, 2, 2 * N], U8)
+        nc.sync.dma_start(w4_raw[:].bitcast(I32), w4_words.rearrange("a p c -> p a c").bitcast(I32))
+        for a in range(2):
+            w1_raw[(a, 1)] = load_w1(a, 1)
 
         gain2 = []
         for i in range(2 * PACK):
-            spread = keep.tile([P, M], F32, name="gain2_%d" % i)
+            spread = keep.tile([P, M], F32, name="gain2_%d" % i, tag="gain2_%d" % i, align_bytes=64)
             column = gain_sb[:, i // PACK, i % PACK : i % PACK + 1]
             nc.scalar.activation(spread[:], column.to_broadcast([P, M]), ACT.Square)
             gain2.append(spread)
@@ -106,11 +111,13 @@ def tile_list_hive_clip_board_kernel(tc, tab_words, tab_scales, offs, pos1, pos2
         w1_sc = {}
 
         def round_w1(a, b):
-            dealt = ring.tile([P, PACK, P, PACK], BF16, name="w1_dealt", align_bytes=64)
+            tag = ("first_turn", "gain2_0")[a] if b else "w1_dealt_%d" % a
+            dealt = keep.tile([P, PACK, P, PACK], BF16, name="w1_dealt_%d%d" % (a, b), tag=tag, align_bytes=64)
+            cut = W1_VECTOR_COLS[b]
             src = w1_raw[(a, b)][:].rearrange("p j (m t) -> p m t j", t=PACK)
             dst = dealt[:].rearrange("p t m j -> p m t j")
-            nc.vector.tensor_copy(dst[:, :W1_VECTOR_COLS], src[:, :W1_VECTOR_COLS])
-            nc.scalar.copy(dst[:, W1_VECTOR_COLS:], src[:, W1_VECTOR_COLS:])
+            nc.vector.tensor_copy(dst[:, :cut], src[:, :cut])
+            nc.scalar.copy(dst[:, cut:], src[:, cut:])
             w1_bf[(a, b)] = dealt
 
         def quantise_w1(a, b, pieces):
@@ -135,14 +142,18 @@ def tile_list_hive_clip_board_kernel(tc, tab_words, tab_scales, offs, pos1, pos2
             w4_raw[:].bitcast(U16).rearrange("p a (g c i t) -> p (a g) c t i", g=2, t=PACK, i=8))
 
         turns, wholes, fracs, sines = {}, {}, {}, {}
-        z_f32 = [keep.tile([P, PACK, M], F32, name="z_f32_%d" % b) for b in range(2)]
+        z_f32 = [keep.tile([P, PACK, M], F32, name="z_f32_0"),
+                 keep.tile([P, PACK, M], F32, name="z_f32_1", tag="table_1", align_bytes=64)]
         z_bf = [keep.tile([P, M, PACK], BF16, name="z_bf_%d" % b, align_bytes=64) for b in range(2)]
         z_codes = [keep.tile([P, M], U32, name="z_codes_%d" % b, align_bytes=64) for b in range(2)]
         z_sc = [keep.tile([P, M], U8, name="z_sc_%d" % b, align_bytes=64) for b in range(2)]
 
         def product1(i):
             b, t = divmod(i, PACK)
-            turn = ring.tile([P, S], F32, name="turn", bufs=3)
+            if i in (0, 2):
+                turn = keep.tile([P, S], F32, name="turn_%d" % i, tag="first_frac" if i else "first_turn", align_bytes=64)
+            else:
+                turn = ring.tile([P, S], F32, name="turn", bufs=3)
             for c in range(0, S, BANK):
                 bank = psum.tile([P, BANK], F32, name="bank")
                 for a in range(2):
@@ -158,9 +169,10 @@ def tile_list_hive_clip_board_kernel(tc, tab_words, tab_scales, offs, pos1, pos2
             turns[i] = turn
 
         def new_tiles(i):
-            wholes[i] = ring.tile([P, S], I32, name="whole")
-            fracs[i] = ring.tile([P, S], F32, name="frac")
-            sines[i] = ring.tile([P, S], F32, name="sine")
+            if i < 2:
+                wholes[i] = keep.tile([P, S], I32, name="whole_%d" % i, tag="first_whole")
+            else:
+                wholes[i] = ring.tile([P, S], I32, name="whole", bufs=3)
 
         def whole_turns(i, cols, on_vector):
             if on_vector:
@@ -175,13 +187,17 @@ def tile_list_hive_clip_board_kernel(tc, tab_words, tab_scales, offs, pos1, pos2
         def sine(i, cols):
             nc.scalar.activation(sines[i][:, cols], fracs[i][:, cols], ACT.Sin, scale=-TWO_PI)
 
-        def pairs(i, lo, hi):
-            b, t = divmod(i, PACK)
-            dusk = ring.tile([P, hi - lo], F32, name="dusk")
-            nc.vector.tensor_tensor(dusk[:], sines[i][:].indirect(pos1_sb[:, lo // 16 : hi // 16]),
+        dusks = {}
+
+        def dusk(i, lo, hi):
+            dusks[(i, lo)] = ring.tile([P, hi - lo], F32, name="dusk", bufs=3)
+            nc.vector.tensor_tensor(dusks[(i, lo)][:], sines[i][:].indirect(pos1_sb[:, lo // 16 : hi // 16]),
                                     gain2[i][:, lo:hi], ALU.mult)
+
+        def dawn(i, lo, hi):
+            b, t = divmod(i, PACK)
             nc.vector.tensor_tensor(z_f32[b][:, t, lo:hi], sines[i][:].indirect(pos2_sb[:, lo // 16 : hi // 16]),
-                                    dusk[:], ALU.mult)
+                                    dusks[(i, lo)][:], ALU.mult)
 
         def weave(copy, dst, src, lo, hi):
             copy(dst[:, lo:hi, :].rearrange("p (c i) t -> p c t i", i=4),
@@ -192,86 +208,127 @@ def tile_list_hive_clip_board_kernel(tc, tab_words, tab_scales, offs, pos1, pos2
                                   src[:, lo:hi, :].rearrange("p m t -> p (m t)"))
 
         everything = slice(0, S)
+        halves = [slice(c, c + BANK) for c in range(0, S, BANK)]
         tiles = 2 * PACK
+
+        def lead(i):
+            product1(i)
+            new_tiles(i)
+            whole_turns(i, everything, False)
+
+        def reduce(i, parts):
+            if i == 0:
+                fracs[i] = keep.tile([P, S], F32, name="frac_0", tag="first_frac", align_bytes=64)
+            else:
+                fracs[i] = ring.tile([P, S], F32, name="frac", bufs=1)
+            for cols in parts:
+                if i == 0:
+                    whole_turns(i, cols, True)
+                fraction(i, cols)
+
         product1(0)
         new_tiles(0)
-        for c in range(0, S, BANK):
-            whole_turns(0, slice(c, c + BANK), True)
-            fraction(0, slice(c, c + BANK))
+        reduce(0, halves)
         for i in range(tiles):
-            if i + 1 < tiles:
-                product1(i + 1)
-                new_tiles(i + 1)
-                whole_turns(i + 1, everything, False)
+            sines[i] = ring.tile([P, S], F32, name="sine")
+            for cols in halves if i == 0 else [everything]:
+                sine(i, cols)
             if i == 0:
-                for c in range(0, S, BANK):
-                    sine(0, slice(c, c + BANK))
-            else:
-                sine(i, everything)
+                round_w1(0, 1)
+                lead(1)
+            if i + 2 < tiles:
+                lead(i + 2)
             if i + 1 < tiles:
-                fraction(i + 1, everything)
-            if i in (0, 1):
-                round_w1(i, 1)
-            if i + 1 < tiles:
-                pairs(i, 0, M)
-            if i in (0, 1):
-                quantise_w1(i, 1, 1)
+                dusk(i, 0, M)
+                if i == 0:
+                    round_w1(1, 1)
+                    quantise_w1(0, 1, 1)
+                reduce(i + 1, [everything])
+                dawn(i, 0, M)
+                if i == 0:
+                    quantise_w1(1, 1, 1)
             if i >= PACK:
                 piece = M // PACK
                 weave(nc.scalar.copy, z_bf[0], z_f32[0], (i - PACK) * piece, (i - PACK + 1) * piece)
-        half = M // 2
-        pairs(tiles - 1, 0, half)
-        weave(nc.scalar.copy, z_bf[1], z_f32[1], 0, half)
+        cuts = [(0, 256), (256, 384), (384, 512)]
         quantise(z_codes[0], z_sc[0], z_bf[0], 0, M)
-        pairs(tiles - 1, half, M)
-        quantise(z_codes[1], z_sc[1], z_bf[1], 0, half)
-        weave(nc.vector.tensor_copy, z_bf[1], z_f32[1], half, M)
-        quantise(z_codes[1], z_sc[1], z_bf[1], half, M)
+        dusk(tiles - 1, *cuts[0])
+        for n, (lo, hi) in enumerate(cuts):
+            if hi < M:
+                dusk(tiles - 1, *cuts[n + 1])
+            dawn(tiles - 1, lo, hi)
+            weave(nc.vector.tensor_copy if hi == M else nc.scalar.copy, z_bf[1], z_f32[1], lo, hi)
+        for lo, hi in (cuts[0], cuts[2], cuts[1]):
+            quantise(z_codes[1], z_sc[1], z_bf[1], lo, hi)
 
-        y_f32 = [keep.tile([P, PACK, J], F32, name="y_f32_%d" % g) for g in range(2)]
+        y_f32 = [keep.tile([P, PACK, J], F32, name="y_f32_%d" % g, tag="w1_raw_%d0" % g) for g in range(2)]
         y_bf = [keep.tile([P, J, PACK], BF16, name="y_bf_%d" % g, align_bytes=64) for g in range(2)]
         y_codes = [keep.tile([P, J], U32, name="y_codes_%d" % g, align_bytes=64) for g in range(2)]
         y_sc = keep.tile([P, 2, J], U8, align_bytes=64)
-        bent, scaled = {}, {}
+        banks, bent, scaled, colonies = {}, {}, {}, {}
 
         def product2(i):
             g, t = divmod(i, PACK)
             bank = psum.tile([P, BANK], F32, name="bank")
             c = g * PASS + t * P
-            for b in range(2):
+            steps = [(0, 0, M)] + [(1, lo, hi) for lo, hi in ((cuts[0], cuts[2], cuts[1]) if i == 0 else [(0, M)])]
+            for n, (b, lo, hi) in enumerate(steps):
                 nc.tensor.matmul_mx(
-                    bank[:],
+                    bank[:, lo:hi],
                     lhsT=w4_dealt[:, b, 2 * c : 2 * (c + P)].bitcast(FP4X4),
                     lhsT_scale=w4_sc[:, b, c : c + P],
-                    rhs=z_codes[b][:].bitcast(FP8X4),
-                    rhs_scale=z_sc[b][:],
-                    start=(b == 0), stop=(b == 1))
+                    rhs=z_codes[b][:, lo:hi].bitcast(FP8X4),
+                    rhs_scale=z_sc[b][:, lo:hi],
+                    start=(n == 0), stop=(n == len(steps) - 1))
             bent[i] = ring.tile([P, M], F32, name="bent", bufs=3)
-            scaled[i] = ring.tile([P, M], F32, name="scaled", bufs=3)
+            banks[i] = bank
             nc.scalar.activation(bent[i][:], bank[:], ACT.Tanh)
-            nc.scalar.activation(scaled[i][:], bank[:], ACT.Copy, scale=sister_sb[:, g, t : t + 1])
 
-        def colonies(i):
+        def scale(i):
             g, t = divmod(i, PACK)
-            colony = ring.tile([P, J], F32, name="colony")
-            nc.vector.tensor_copy(colony[:], bent[i][:].indirect(pos3_sb[:]))
-            nc.vector.tensor_tensor(y_f32[g][:, t, :], scaled[i][:].indirect(pos4_sb[:]), colony[:], ALU.add)
+            scaled[i] = ring.tile([P, M], F32, name="scaled", bufs=3)
+            nc.scalar.activation(scaled[i][:], banks[i][:], ACT.Copy, scale=sister_sb[:, g, t : t + 1])
+
+        def colony(i):
+            colonies[i] = ring.tile([P, J], F32, name="colony", bufs=3)
+            nc.vector.tensor_copy(colonies[i][:], bent[i][:].indirect(pos3_sb[:]))
+
+        def add_sister(i, lo, hi):
+            g, t = divmod(i, PACK)
+            nc.vector.tensor_tensor(y_f32[g][:, t, lo:hi], scaled[i][:].indirect(pos4_sb[:, lo // 16 : hi // 16]),
+                                    colonies[i][:, lo:hi], ALU.add)
+
+        def store_rows(i):
+            g, t = divmod(i, PACK)
             rows = out_0[g * PASS : (g + 1) * PASS, :].rearrange("(p t) j -> p t j", t=PACK)
             nc.sync.dma_start(rows[:, t, :], y_f32[g][:, t, :])
 
-        def planes(g, copy):
-            weave(copy, y_bf[g], y_f32[g], 0, J)
-            quantise(y_codes[g], y_sc[:, g, :], y_bf[g], 0, J)
+        def store_words(g):
             nc.sync.dma_start(out_1[g].rearrange("p m t -> p (m t)").bitcast(I32), y_codes[g][:].bitcast(I32))
 
         product2(0)
-        for i in range(tiles):
-            if i + 1 < tiles:
-                product2(i + 1)
-            colonies(i)
+        colony(0)
+        for i in range(tiles - 1):
+            product2(i + 1)
+            scale(i)
+            colony(i + 1)
+            add_sister(i, 0, J)
+            store_rows(i)
             if i == PACK:
-                planes(0, nc.scalar.copy)
-        planes(1, nc.vector.tensor_copy)
+                weave(nc.scalar.copy, y_bf[0], y_f32[0], 0, J)
+            if i == PACK + 1:
+                quantise(y_codes[0], y_sc[:, 0, :], y_bf[0], 0, J)
+                store_words(0)
+        half = J // 2
+        scale(tiles - 1)
+        add_sister(tiles - 1, 0, half)
+        weave(nc.scalar.copy, y_bf[1], y_f32[1], 0, half)
+        add_sister(tiles - 1, half, J)
+        store_rows(tiles - 1)
+        weave(nc.vector.tensor_copy, y_bf[1], y_f32[1], half, J)
+        quantise(y_codes[1], y_sc[:, 1, :], y_bf[1], 0, half)
+        quantise(y_codes[1], y_sc[:, 1, :], y_bf[1], half, J)
+        store_words(1)
         for q in range(QUADS):
             queue = nc.scalar if q % 2 else nc.sync
             queue.dma_start(out_2[:, 4 * q : 4 * q + 4, :].rearrange("g r m -> r g m").bitcast(I32),

@@ -22,9 +22,10 @@ PACK = 4
 PASS = P * PACK
 BANK = 512
 QUADS = 4
+QUADRANT_ORDER = (0, 2, 1, 3)
 TWO_PI = 2.0 * math.pi
 ROUNDER = 1.5 * 2.0**23
-W1_VECTOR_COLS = (88, 96)
+W1_VECTOR_COLS = (80, 96)
 
 
 def tile_list_hive_clip_board_kernel(tc, tab_words, tab_scales, offs, pos1, pos2, pos3, pos4, w1, b1, gain,
@@ -71,12 +72,12 @@ def tile_list_hive_clip_board_kernel(tc, tab_words, tab_scales, offs, pos1, pos2
         load_table(0, 0)
         pos3_sb = load_list(pos3, "pos3_sb")
         pos4_sb = load_list(pos4, "pos4_sb")
-        for q in range(QUADS):
+        for q in QUADRANT_ORDER:
             nc.sync.dma_start(table_sc[32 * q : 32 * q + 8, :].bitcast(I32),
                               tab_scales[:, 4 * q : 4 * q + 4, :].bitcast(I32))
         load_table(0, 1)
         load_table(1, 0)
-        for q in range(QUADS):
+        for q in QUADRANT_ORDER:
             nc.sync.dma_start(w4_sc_raw[32 * q : 32 * q + 4, :, :].bitcast(I32),
                               w4_scales[:, 4 * q : 4 * q + 4, :].rearrange("a r n -> r a n").bitcast(I32))
         load_table(1, 1)
@@ -86,6 +87,8 @@ def tile_list_hive_clip_board_kernel(tc, tab_words, tab_scales, offs, pos1, pos2
         for a in range(2):
             w1_raw[(a, 1)] = load_w1(a, 1)
 
+        warm = keep.tile([P, 1], F32)
+        nc.scalar.activation(warm[:], gain_sb[:, 0, 0:1], ACT.Silu)
         gain2 = []
         for i in range(2 * PACK):
             spread = keep.tile([P, M], F32, name="gain2_%d" % i, tag="gain2_%d" % i, align_bytes=64)
@@ -153,7 +156,7 @@ def tile_list_hive_clip_board_kernel(tc, tab_words, tab_scales, offs, pos1, pos2
             if i in (0, 2):
                 turn = keep.tile([P, S], F32, name="turn_%d" % i, tag="first_frac" if i else "first_turn", align_bytes=64)
             else:
-                turn = ring.tile([P, S], F32, name="turn", bufs=3)
+                turn = ring.tile([P, S], F32, name="turn", bufs=2)
             for c in range(0, S, BANK):
                 bank = psum.tile([P, BANK], F32, name="bank")
                 for a in range(2):
@@ -172,7 +175,7 @@ def tile_list_hive_clip_board_kernel(tc, tab_words, tab_scales, offs, pos1, pos2
             if i < 2:
                 wholes[i] = keep.tile([P, S], I32, name="whole_%d" % i, tag="first_whole")
             else:
-                wholes[i] = ring.tile([P, S], I32, name="whole", bufs=3)
+                wholes[i] = ring.tile([P, S], I32, name="whole", bufs=2)
 
         def whole_turns(i, cols, on_vector):
             if on_vector:
@@ -190,7 +193,7 @@ def tile_list_hive_clip_board_kernel(tc, tab_words, tab_scales, offs, pos1, pos2
         dusks = {}
 
         def dusk(i, lo, hi):
-            dusks[(i, lo)] = ring.tile([P, hi - lo], F32, name="dusk", bufs=3)
+            dusks[(i, lo)] = ring.tile([P, hi - lo], F32, name="dusk", bufs=4)
             nc.vector.tensor_tensor(dusks[(i, lo)][:], sines[i][:].indirect(pos1_sb[:, lo // 16 : hi // 16]),
                                     gain2[i][:, lo:hi], ALU.mult)
 
@@ -220,7 +223,7 @@ def tile_list_hive_clip_board_kernel(tc, tab_words, tab_scales, offs, pos1, pos2
             if i == 0:
                 fracs[i] = keep.tile([P, S], F32, name="frac_0", tag="first_frac", align_bytes=64)
             else:
-                fracs[i] = ring.tile([P, S], F32, name="frac", bufs=1)
+                fracs[i] = ring.tile([P, S], F32, name="frac", bufs=2)
             for cols in parts:
                 if i == 0:
                     whole_turns(i, cols, True)
@@ -230,21 +233,26 @@ def tile_list_hive_clip_board_kernel(tc, tab_words, tab_scales, offs, pos1, pos2
         new_tiles(0)
         reduce(0, halves)
         for i in range(tiles):
-            sines[i] = ring.tile([P, S], F32, name="sine")
+            if 0 < i < tiles - 2:
+                lead(i + 2)
+            sines[i] = ring.tile([P, S], F32, name="sine", bufs=2)
             for cols in halves if i == 0 else [everything]:
                 sine(i, cols)
             if i == 0:
                 round_w1(0, 1)
                 lead(1)
-            if i + 2 < tiles:
-                lead(i + 2)
+                reduce(1, [everything])
+                lead(2)
             if i + 1 < tiles:
-                dusk(i, 0, M)
+                dusk(i, 0, M // 2)
+                dusk(i, M // 2, M)
                 if i == 0:
                     round_w1(1, 1)
                     quantise_w1(0, 1, 1)
-                reduce(i + 1, [everything])
-                dawn(i, 0, M)
+                if i + 2 < tiles:
+                    reduce(i + 2, [everything])
+                dawn(i, 0, M // 2)
+                dawn(i, M // 2, M)
                 if i == 0:
                     quantise_w1(1, 1, 1)
             if i >= PACK:
@@ -280,13 +288,13 @@ def tile_list_hive_clip_board_kernel(tc, tab_words, tab_scales, offs, pos1, pos2
                     rhs=z_codes[b][:, lo:hi].bitcast(FP8X4),
                     rhs_scale=z_sc[b][:, lo:hi],
                     start=(n == 0), stop=(n == len(steps) - 1))
-            bent[i] = ring.tile([P, M], F32, name="bent", bufs=3)
+            bent[i] = ring.tile([P, M], F32, name="bent", bufs=4)
             banks[i] = bank
             nc.scalar.activation(bent[i][:], bank[:], ACT.Tanh)
 
         def scale(i):
             g, t = divmod(i, PACK)
-            scaled[i] = ring.tile([P, M], F32, name="scaled", bufs=3)
+            scaled[i] = ring.tile([P, M], F32, name="scaled", bufs=4)
             nc.scalar.activation(scaled[i][:], banks[i][:], ACT.Copy, scale=sister_sb[:, g, t : t + 1])
 
         def colony(i):
@@ -314,16 +322,14 @@ def tile_list_hive_clip_board_kernel(tc, tab_words, tab_scales, offs, pos1, pos2
             colony(i + 1)
             add_sister(i, 0, J)
             store_rows(i)
-            if i == PACK:
-                weave(nc.scalar.copy, y_bf[0], y_f32[0], 0, J)
-            if i == PACK + 1:
-                quantise(y_codes[0], y_sc[:, 0, :], y_bf[0], 0, J)
-                store_words(0)
         half = J // 2
+        weave(nc.scalar.copy, y_bf[0], y_f32[0], 0, J)
         scale(tiles - 1)
         add_sister(tiles - 1, 0, half)
         weave(nc.scalar.copy, y_bf[1], y_f32[1], 0, half)
         add_sister(tiles - 1, half, J)
+        quantise(y_codes[0], y_sc[:, 0, :], y_bf[0], 0, J)
+        store_words(0)
         store_rows(tiles - 1)
         weave(nc.vector.tensor_copy, y_bf[1], y_f32[1], half, J)
         quantise(y_codes[1], y_sc[:, 1, :], y_bf[1], 0, half)

@@ -117,8 +117,8 @@ def tile_list_hive_clip_board_kernel(tc, tab_words, tab_scales, offs, pos1, pos2
             tag = ("first_turn", "gain2_0")[a] if b else "w1_dealt_%d" % a
             dealt = keep.tile([P, PACK, P, PACK], BF16, name="w1_dealt_%d%d" % (a, b), tag=tag, align_bytes=64)
             cut = W1_VECTOR_COLS[b]
-            src = w1_raw[(a, b)][:].rearrange("p j (m t) -> p m t j", t=PACK)
-            dst = dealt[:].rearrange("p t m j -> p m t j")
+            src = w1_raw[(a, b)][:].rearrange("p j (m t) -> p m j t", t=PACK)
+            dst = dealt[:].rearrange("p t m j -> p m j t")
             nc.vector.tensor_copy(dst[:, :cut], src[:, :cut])
             nc.scalar.copy(dst[:, cut:], src[:, cut:])
             w1_bf[(a, b)] = dealt
@@ -224,9 +224,10 @@ def tile_list_hive_clip_board_kernel(tc, tab_words, tab_scales, offs, pos1, pos2
                 fracs[i] = keep.tile([P, S], F32, name="frac_0", tag="first_frac", align_bytes=64)
             else:
                 fracs[i] = ring.tile([P, S], F32, name="frac", bufs=2)
-            for cols in parts:
-                if i == 0:
+            if i == 0:
+                for cols in parts:
                     whole_turns(i, cols, True)
+            for cols in parts:
                 fraction(i, cols)
 
         product1(0)

import math
from contextlib import ExitStack

import concourse.mybir as mybir

K, T, S, H, M, N, J = 1024, 4096, 1024, 1024, 512, 1024, 256
FLOPS = 2 * K * H * S + 2 * H * N * M

F32 = mybir.dt.float32
BF16 = mybir.dt.bfloat16
I32 = mybir.dt.int32
U32 = mybir.dt.uint32
U16 = mybir.dt.uint16
U8 = mybir.dt.uint8
FP8X4 = mybir.dt.float8_e4m3fn_x4
FP4X4 = mybir.dt.float4_e2m1fn_x4
ACT = mybir.ActivationFunctionType
ALU = mybir.AluOpType

P = 128
PACK = 4
PASS = P * PACK
BANK = 512
QUADS = 4
QUADRANT_ORDER = (0, 2, 1, 3)
TWO_PI = 2.0 * math.pi
ROUNDER = 1.5 * 2.0**23
W1_VECTOR_COLS = (80, 96)


def tile_list_hive_clip_board_kernel(tc, tab_words, tab_scales, offs, pos1, pos2, pos3, pos4, w1, b1, gain,
                                                w4_words, w4_scales, sister, out_0, out_1, out_2):
    nc = tc.nc
    with ExitStack() as ctx:
        keep = ctx.enter_context(tc.tile_pool(name="keep", bufs=1))
        ring = ctx.enter_context(tc.tile_pool(name="ring", bufs=2))
        psum = ctx.enter_context(tc.psum_pool(name="psum", bufs=8))

        def load_list(src, name):
            tile = keep.tile(list(src.shape), U16, name=name)
            nc.sync.dma_start(tile[:], src)
            return tile

        def load_rows(src, name):
            tile = keep.tile([P, 2, PACK], F32, name=name)
            nc.sync.dma_start(tile[:], src.rearrange("(b p t) -> p b t", p=P, t=PACK))
            return tile

        def load_table(a, half):
            cols = slice(half * T // 2, (half + 1) * T // 2)
            nc.sync.dma_start(table[a][:, cols], tab_words[a].rearrange("p t i -> p (t i)").bitcast(I32)[:, cols])

        def load_w1(a, b):
            raw = keep.tile([P, PACK, PASS], F32, name="w1_raw_%d%d" % (a, b), tag="w1_raw_%d%d" % (a, b))
            rows = w1[a * PASS : (a + 1) * PASS, b * PASS : (b + 1) * PASS]
            nc.sync.dma_start(raw[:], rows.rearrange("(p j) c -> p j c", j=PACK))
            return raw

        table_sc = keep.tile([P, T], U8)
        w4_sc_raw = keep.tile([P, 2, N], U8)
        nc.vector.memset(table_sc[:, : T // 2].bitcast(I32), 0)
        nc.gpsimd.memset(table_sc[:, T // 2 :].bitcast(I32), 0)
        nc.vector.memset(w4_sc_raw[:].bitcast(I32), 0)
        table = [keep.tile([P, T], I32, name="table_%d" % a, tag="table_%d" % a, align_bytes=64) for a in range(2)]
        w1_raw = {(0, 0): load_w1(0, 0)}
        offs_sb = load_list(offs, "offs_sb")
        gain_sb = load_rows(gain, "gain_sb")
        b1_sb = load_rows(b1, "b1_sb")
        sister_sb = load_rows(sister, "sister_sb")
        pos1_sb = load_list(pos1, "pos1_sb")
        pos2_sb = load_list(pos2, "pos2_sb")
        load_table(0, 0)
        pos3_sb = load_list(pos3, "pos3_sb")
        pos4_sb = load_list(pos4, "pos4_sb")
        for q in QUADRANT_ORDER:
            nc.sync.dma_start(table_sc[32 * q : 32 * q + 8, :].bitcast(I32),
                              tab_scales[:, 4 * q : 4 * q + 4, :].bitcast(I32))
        load_table(0, 1)
        load_table(1, 0)
        for q in QUADRANT_ORDER:
            nc.sync.dma_start(w4_sc_raw[32 * q : 32 * q + 4, :, :].bitcast(I32),
                              w4_scales[:, 4 * q : 4 * q + 4, :].rearrange("a r n -> r a n").bitcast(I32))
        load_table(1, 1)
        w1_raw[(1, 0)] = load_w1(1, 0)
        w4_raw = keep.tile([P, 2, 2 * N], U8)
        nc.sync.dma_start(w4_raw[:].bitcast(I32), w4_words.rearrange("a p c -> p a c").bitcast(I32))
        for a in range(2):
            w1_raw[(a, 1)] = load_w1(a, 1)

        warm = keep.tile([P, 1], F32)
        nc.scalar.activation(warm[:], gain_sb[:, 0, 0:1], ACT.Silu)
        gain2 = []
        for i in range(2 * PACK):
            spread = keep.tile([P, M], F32, name="gain2_%d" % i, tag="gain2_%d" % i, align_bytes=64)
            column = gain_sb[:, i // PACK, i % PACK : i % PACK + 1]
            nc.scalar.activation(spread[:], column.to_broadcast([P, M]), ACT.Square)
            gain2.append(spread)
        b1_turns = keep.tile([P, 2, PACK], F32)
        nc.scalar.activation(b1_turns[:], b1_sb[:], ACT.Copy, scale=1.0 / TWO_PI)

        picked = [keep.tile([P, S], U32, name="picked_%d" % a, align_bytes=64) for a in range(2)]
        picked_sc = keep.tile([P, S], U8, align_bytes=64)
        nc.vector.tensor_copy(picked[0][:], table[0][:].bitcast(U32).indirect(offs_sb[:]))
        nc.vector.tensor_copy(picked_sc[:], table_sc[:].indirect(offs_sb[:]))
        nc.vector.tensor_copy(picked[1][:], table[1][:].bitcast(U32).indirect(offs_sb[:]))

        w4_sc = keep.tile([P, 2, N], U8, align_bytes=64)
        nc.vector.tensor_copy(
            w4_sc[:].rearrange("p a (g t c i) -> p (a g) c t i", g=2, t=PACK, i=16),
            w4_sc_raw[:].rearrange("p a (g c i t) -> p (a g) c t i", g=2, t=PACK, i=16))

        w1_bf = {}
        w1_codes = {}
        w1_sc = {}

        def round_w1(a, b):
            tag = ("first_turn", "gain2_0")[a] if b else "w1_dealt_%d" % a
            dealt = keep.tile([P, PACK, P, PACK], BF16, name="w1_dealt_%d%d" % (a, b), tag=tag, align_bytes=64)
            cut = W1_VECTOR_COLS[b]
            src = w1_raw[(a, b)][:].rearrange("p j (m t) -> p m j t", t=PACK)
            dst = dealt[:].rearrange("p t m j -> p m j t")
            nc.vector.tensor_copy(dst[:, :cut], src[:, :cut])
            nc.scalar.copy(dst[:, cut:], src[:, cut:])
            w1_bf[(a, b)] = dealt

        def quantise_w1(a, b, pieces):
            codes = keep.tile([P, PASS], U32, name="w1_codes_%d%d" % (a, b), align_bytes=64)
            scales = keep.tile([P, PASS], U8, name="w1_sc_%d%d" % (a, b), align_bytes=64)
            flat = w1_bf[(a, b)][:].rearrange("p t m j -> p (t m j)")
            width = PASS // pieces
            for c in range(0, PASS, width):
                nc.vector.quantize_mx(codes[:, c : c + width].bitcast(FP8X4), scales[:, c : c + width],
                                      flat[:, PACK * c : PACK * (c + width)])
            w1_codes[(a, b)] = codes
            w1_sc[(a, b)] = scales

        round_w1(0, 0)
        quantise_w1(0, 0, 1)
        round_w1(1, 0)
        quantise_w1(1, 0, PACK)

        w4_dealt = keep.tile([P, 2, 2 * N], U8, align_bytes=64)
        nc.vector.tensor_copy(
            w4_dealt[:].bitcast(U16).rearrange("p a (g t c i) -> p (a g) c t i", g=2, t=PACK, i=8),
            w4_raw[:].bitcast(U16).rearrange("p a (g c i t) -> p (a g) c t i", g=2, t=PACK, i=8))

        turns, wholes, fracs, sines = {}, {}, {}, {}
        z_f32 = [keep.tile([P, PACK, M], F32, name="z_f32_0"),
                 keep.tile([P, PACK, M], F32, name="z_f32_1", tag="table_1", align_bytes=64)]
        z_bf = [keep.tile([P, M, PACK], BF16, name="z_bf_%d" % b, align_bytes=64) for b in range(2)]
        z_codes = [keep.tile([P, M], U32, name="z_codes_%d" % b, align_bytes=64) for b in range(2)]
        z_sc = [keep.tile([P, M], U8, name="z_sc_%d" % b, align_bytes=64) for b in range(2)]

        def product1(i):
            b, t = divmod(i, PACK)
            if i in (0, 2):
                turn = keep.tile([P, S], F32, name="turn_%d" % i, tag="first_frac" if i else "first_turn", align_bytes=64)
            else:
                turn = ring.tile([P, S], F32, name="turn", bufs=2)
            for c in range(0, S, BANK):
                bank = psum.tile([P, BANK], F32, name="bank")
                for a in range(2):
                    nc.tensor.matmul_mx(
                        bank[:],
                        lhsT=w1_codes[(a, b)][:, t * P : (t + 1) * P].bitcast(FP8X4),
                        lhsT_scale=w1_sc[(a, b)][:, t * P : (t + 1) * P],
                        rhs=picked[a][:, c : c + BANK].bitcast(FP8X4),
                        rhs_scale=picked_sc[4 * a :, c : c + BANK],
                        start=(a == 0), stop=(a == 1))
                nc.scalar.activation(turn[:, c : c + BANK], bank[:], ACT.Identity,
                                     bias=b1_turns[:, b, t : t + 1], scale=1.0 / TWO_PI)
            turns[i] = turn

        def new_tiles(i):
            if i < 2:
                wholes[i] = keep.tile([P, S], I32, name="whole_%d" % i, tag="first_whole")
            else:
                wholes[i] = ring.tile([P, S], I32, name="whole", bufs=2)

        def whole_turns(i, cols, on_vector):
            if on_vector:
                nc.vector.tensor_scalar(wholes[i][:, cols], turns[i][:, cols], ROUNDER, None, ALU.add)
            else:
                nc.scalar.activation(wholes[i][:, cols].bitcast(U32), turns[i][:, cols], ACT.Copy, bias=ROUNDER)

        def fraction(i, cols):
            nc.vector.scalar_tensor_tensor(fracs[i][:, cols], wholes[i][:, cols], ROUNDER, turns[i][:, cols],
                                           ALU.subtract, ALU.subtract)

        def sine(i, cols):
            nc.scalar.activation(sines[i][:, cols], fracs[i][:, cols], ACT.Sin, scale=-TWO_PI)

        dusks = {}

        def dusk(i, lo, hi):
            dusks[(i, lo)] = ring.tile([P, hi - lo], F32, name="dusk", bufs=4)
            nc.vector.tensor_tensor(dusks[(i, lo)][:], sines[i][:].indirect(pos1_sb[:, lo // 16 : hi // 16]),
                                    gain2[i][:, lo:hi], ALU.mult)

        def dawn(i, lo, hi):
            b, t = divmod(i, PACK)
            nc.vector.tensor_tensor(z_f32[b][:, t, lo:hi], sines[i][:].indirect(pos2_sb[:, lo // 16 : hi // 16]),
                                    dusks[(i, lo)][:], ALU.mult)

        def weave(copy, dst, src, lo, hi):
            copy(dst[:, lo:hi, :].rearrange("p (c i) t -> p c t i", i=4),
                 src[:, :, lo:hi].rearrange("p t (c i) -> p c t i", i=4))

        def quantise(codes, scales, src, lo, hi):
            nc.vector.quantize_mx(codes[:, lo:hi].bitcast(FP8X4), scales[:, lo:hi],
                                  src[:, lo:hi, :].rearrange("p m t -> p (m t)"))

        everything = slice(0, S)
        halves = [slice(c, c + BANK) for c in range(0, S, BANK)]
        tiles = 2 * PACK

        def lead(i):
            product1(i)
            new_tiles(i)
            whole_turns(i, everything, False)

        def reduce(i, parts):
            if i == 0:
                fracs[i] = keep.tile([P, S], F32, name="frac_0", tag="first_frac", align_bytes=64)
            else:
                fracs[i] = ring.tile([P, S], F32, name="frac", bufs=2)
            if i == 0:
                for cols in parts:
                    whole_turns(i, cols, True)
            for cols in parts:
                fraction(i, cols)

        product1(0)
        new_tiles(0)
        reduce(0, halves)
        for i in range(tiles):
            if 0 < i < tiles - 2:
                lead(i + 2)
            sines[i] = ring.tile([P, S], F32, name="sine", bufs=2)
            for cols in halves if i == 0 else [everything]:
                sine(i, cols)
            if i == 0:
                round_w1(0, 1)
                lead(1)
                reduce(1, [everything])
                lead(2)
            if i + 1 < tiles:
                dusk(i, 0, M // 2)
                dusk(i, M // 2, M)
                if i == 0:
                    round_w1(1, 1)
                    quantise_w1(0, 1, 1)
                if i + 2 < tiles:
                    reduce(i + 2, [everything])
                dawn(i, 0, M // 2)
                dawn(i, M // 2, M)
                if i == 0:
                    quantise_w1(1, 1, 1)
            if i >= PACK:
                piece = M // PACK
                weave(nc.scalar.copy, z_bf[0], z_f32[0], (i - PACK) * piece, (i - PACK + 1) * piece)
        cuts = [(0, 256), (256, 384), (384, 512)]
        quantise(z_codes[0], z_sc[0], z_bf[0], 0, M)
        dusk(tiles - 1, *cuts[0])
        for n, (lo, hi) in enumerate(cuts):
            if hi < M:
                dusk(tiles - 1, *cuts[n + 1])
            dawn(tiles - 1, lo, hi)
            weave(nc.vector.tensor_copy if hi == M else nc.scalar.copy, z_bf[1], z_f32[1], lo, hi)
        for lo, hi in (cuts[0], cuts[2], cuts[1]):
            quantise(z_codes[1], z_sc[1], z_bf[1], lo, hi)

        y_f32 = [keep.tile([P, PACK, J], F32, name="y_f32_%d" % g, tag="w1_raw_%d0" % g) for g in range(2)]
        y_bf = [keep.tile([P, J, PACK], BF16, name="y_bf_%d" % g, align_bytes=64) for g in range(2)]
        y_codes = [keep.tile([P, J], U32, name="y_codes_%d" % g, align_bytes=64) for g in range(2)]
        y_sc = keep.tile([P, 2, J], U8, align_bytes=64)
        banks, bent, scaled, colonies = {}, {}, {}, {}

        def product2(i):
            g, t = divmod(i, PACK)
            bank = psum.tile([P, BANK], F32, name="bank")
            c = g * PASS + t * P
            steps = [(0, 0, M)] + [(1, lo, hi) for lo, hi in ((cuts[0], cuts[2], cuts[1]) if i == 0 else [(0, M)])]
            for n, (b, lo, hi) in enumerate(steps):
                nc.tensor.matmul_mx(
                    bank[:, lo:hi],
                    lhsT=w4_dealt[:, b, 2 * c : 2 * (c + P)].bitcast(FP4X4),
                    lhsT_scale=w4_sc[:, b, c : c + P],
                    rhs=z_codes[b][:, lo:hi].bitcast(FP8X4),
                    rhs_scale=z_sc[b][:, lo:hi],
                    start=(n == 0), stop=(n == len(steps) - 1))
            bent[i] = ring.tile([P, M], F32, name="bent", bufs=4)
            banks[i] = bank
            nc.scalar.activation(bent[i][:], bank[:], ACT.Tanh)

        def scale(i):
            g, t = divmod(i, PACK)
            scaled[i] = ring.tile([P, M], F32, name="scaled", bufs=4)
            nc.scalar.activation(scaled[i][:], banks[i][:], ACT.Copy, scale=sister_sb[:, g, t : t + 1])

        def colony(i):
            colonies[i] = ring.tile([P, J], F32, name="colony", bufs=3)
            nc.vector.tensor_copy(colonies[i][:], bent[i][:].indirect(pos3_sb[:]))

        def add_sister(i, lo, hi):
            g, t = divmod(i, PACK)
            nc.vector.tensor_tensor(y_f32[g][:, t, lo:hi], scaled[i][:].indirect(pos4_sb[:, lo // 16 : hi // 16]),
                                    colonies[i][:, lo:hi], ALU.add)

        def store_rows(i):
            g, t = divmod(i, PACK)
            rows = out_0[g * PASS : (g + 1) * PASS, :].rearrange("(p t) j -> p t j", t=PACK)
            nc.sync.dma_start(rows[:, t, :], y_f32[g][:, t, :])

        def store_words(g):
            nc.sync.dma_start(out_1[g].rearrange("p m t -> p (m t)").bitcast(I32), y_codes[g][:].bitcast(I32))

        product2(0)
        colony(0)
        for i in range(tiles - 1):
            product2(i + 1)
            scale(i)
            colony(i + 1)
            add_sister(i, 0, J)
            store_rows(i)
        half = J // 2
        weave(nc.scalar.copy, y_bf[0], y_f32[0], 0, J)
        scale(tiles - 1)
        add_sister(tiles - 1, 0, half)
        weave(nc.scalar.copy, y_bf[1], y_f32[1], 0, half)
        add_sister(tiles - 1, half, J)
        quantise(y_codes[0], y_sc[:, 0, :], y_bf[0], 0, J)
        store_words(0)
        store_rows(tiles - 1)
        weave(nc.vector.tensor_copy, y_bf[1], y_f32[1], half, J)
        quantise(y_codes[1], y_sc[:, 1, :], y_bf[1], 0, half)
        quantise(y_codes[1], y_sc[:, 1, :], y_bf[1], half, J)
        store_words(1)
        for q in range(QUADS):
            queue = nc.scalar if q % 2 else nc.sync
            queue.dma_start(out_2[:, 4 * q : 4 * q + 4, :].rearrange("g r m -> r g m").bitcast(I32),
                            y_sc[32 * q : 32 * q + 4, :, :].bitcast(I32))
